import numpy as np, ml_dtypes
CORES = [16,23,24,31,64,71]
N = 6
KB, QP = 1, 32
WB = 1
def setup_inputs(rng):
    q = rng.standard_normal((N, 128, QP), dtype=np.float32) / 4; k = rng.standard_normal((N, 128, KB * 128), dtype=np.float32)
    a = 2 * np.pi * rng.random((N, QP)); s = 400 * rng.random((N, QP)) ** 1.5; q[:, 0, :] = s * np.cos(a); q[:, 1, :] = s * np.sin(a); q[:, 2, :] = 150 * rng.standard_normal((N, QP)); k[:, 2, :] = 1 + k[:, 2, :] / 50
    a = (2 * np.pi * rng.random() + np.pi / 2 * (rng.permutation(N).reshape(N, 1, 1) + 0.5) / N - 0.5 + (np.arange(KB).reshape(1, KB, 1) + rng.random((N, KB, 128))) / KB).reshape(N, KB * 128); k[:, 0, :] = np.cos(a); k[:, 1, :] = np.sin(a)
    return {"q": q.astype(ml_dtypes.bfloat16), "k": k.astype(ml_dtypes.bfloat16), "v": rng.standard_normal((N, 128, KB * 128), dtype=np.float32).astype(ml_dtypes.bfloat16)}
def setup_inputs_big(rng):
    d = setup_inputs(rng)
    for k in ("v",): d[k] = (d[k].astype(np.float32) * 1048576.0).astype(d[k].dtype)
    return d
def setup_inputs_small(rng):
    d = setup_inputs(rng)
    for k in ("v",): d[k] = (d[k].astype(np.float32) * (1 / 1048576.0)).astype(d[k].dtype)
    return d
def reference(q, k, v):
    Q, K, V = q.astype(np.float64), k.astype(np.float64), v.astype(np.float64)
    y = np.zeros((N, QP, 128))
    for r in range(N):
        js = list(range(max(0, r - WB), r + 1))
        S = np.concatenate([K[j].T @ Q[r] for j in js], axis=0)
        P = np.exp(S - S.max(axis=0)); P = P / P.sum(axis=0)
        y[r] = P.T @ np.concatenate([V[j][:, 128 * b:128 * b + 128] for j in js for b in range(KB)], axis=0)
    return {"y": y.astype(ml_dtypes.bfloat16)}

@@ -1,0 +1,144 @@
+from concourse.mybir import AluOpType, AxisListType, ActivationFunctionType
+
+QP = 32
+KP = 128
+NG = KP // QP
+W = 2 * KP
+SEND_ENGINES = 8
+FAR = -30000.0
+
+SCRATCH = {
+    "kvo": ("sbuf", [128, W + 8], "bfloat16"),
+    "kvp": ("sbuf", [128, W + 8], "bfloat16"),
+    "q4": ("sbuf", [128, NG * QP], "bfloat16"),
+    "z": ("sbuf", [128, 8], "bfloat16"),
+    "nmask": ("sbuf", [128, QP], "float32"),
+    "nm1": ("sbuf", [128, 4], "float32"),
+    "nm": ("sbuf", [128, 4], "float32"),
+    "p1q": ("sbuf", [128, QP], "bfloat16"),
+    "p1t": ("sbuf", [128, QP], "bfloat16"),
+    "pq": ("sbuf", [128, 2 * QP], "bfloat16"),
+    "pt": ("sbuf", [128, QP], "bfloat16"),
+    "o1b": ("sbuf", [128, KP + 8], "bfloat16"),
+    "rl": ("sbuf", [128, 4], "float32"),
+    "ysb": ("sbuf", [128, KP], "bfloat16"),
+    "so": ("psum", [128, 512], "float32"),
+    "sco": ("psum", [128, 512], "float32"),
+    "sp": ("psum", [128, 512], "float32"),
+    "scp": ("psum", [128, 512], "float32"),
+    "o1": ("psum", [128, 512], "float32"),
+    "o": ("psum", [128, 512], "float32"),
+}
+SEMAPHORES = ["kv", "q", "z", "nm0", "nmask", "ones", "q4", "so", "sco", "nm1", "pre", "p1q", "p1t", "o1", "o1b",
+              "arr", "sent", "sp", "scp", "nm", "pq", "pt", "o", "rl", "y", "st"]
+
+
+def _engines(mask, n):
+    out, cnt = 0, 0
+    for b in range(mask.bit_length()):
+        if (mask >> b) & 1 and cnt < n:
+            out |= 1 << b
+            cnt += 1
+    return out, cnt
+
+
+def rank_program(g, core, T, topo):
+    rank = T.rank_of(core)
+    if rank is None:
+        return
+    S = T.sem
+    pe, dve, act, sp = g.tensor, g.vector, g.scalar, g.sync
+    Exp = ActivationFunctionType.Exp
+    X = AxisListType.X
+    n = len(T.cores)
+    has_prev = rank > 0
+    has_next = rank + 1 < n
+
+    sp.dma_start(T.kvo[:, 0:KP], T.k[:, :]).then_inc(S.kv, 16)
+    act.dma_start(T.kvo[:, KP:W], T.v[:, :]).then_inc(S.kv, 16)
+    sp.dma_start(T.q4[:, 0:QP], T.q[:, :]).then_inc(S.q, 16)
+
+    dve.memset(T.z[:, :], 0.0).then_inc(S.z, 1)
+    act.wait_ge(S.z, 1)
+    act.activation(T.kvo[:, W:W + 8], T.z[:, :], Exp).then_inc(S.ones, 1)
+    n_ones = 1
+    if has_prev:
+        act.activation(T.kvp[:, W:W + 8], T.z[:, :], Exp).then_inc(S.ones, 1)
+        n_ones = 2
+        dve.memset(T.nmask[:, :], 0.0).then_inc(S.nm0, 1)
+        g.wait_ge(S.nm0, 1)
+        g.affine_select(T.nmask[:, :], T.nmask[:, :], [[-1, QP]], AluOpType.is_equal, FAR, 0, 1).then_inc(S.nmask, 1)
+
+    if has_next:
+        dst = T.cores[rank + 1]
+        if not topo.may_write(core, dst):
+            raise ValueError("rank %d may not write to the next rank directly" % rank)
+        rid, pid, _ = topo.addr(dst)
+        em, ne = _engines(topo.mask(core, dst), SEND_ENGINES)
+        g.wait_ge(S.kv, 32)
+        g.remote_dma(T.kvp[:, 0:W], T.kvo[:, 0:W], S.arr, S.sent, pid, rid, em)
+        g.wait_ge(S.sent, ne)
+
+    dve.wait_ge(S.q, 16)
+    for a in range(1, NG):
+        dve.tensor_copy(T.q4[:, a * QP:(a + 1) * QP], T.q4[:, 0:QP]).then_inc(S.q4, 1)
+    pe.wait_ge(S.kv, 32)
+    pe.wait_ge(S.q, 16)
+    pe.wait_ge(S.q4, NG - 1)
+    pe.matmul(T.so[:, 0:KP], T.q4[:, :], T.kvo[:, 0:KP], True, True).then_inc(S.so, 1)
+    for a in range(NG):
+        pe.matmul(T.sco[a * QP:(a + 1) * QP, 0:QP], T.q4[:, 0:QP], T.kvo[:, a * QP:(a + 1) * QP],
+                  True, True).then_inc(S.sco, 1)
+    dve.wait_ge(S.so, 1)
+    dve.tensor_reduce(T.nm1[:, 0:1], T.so[:, 0:KP], X, AluOpType.max, negate=True).then_inc(S.nm1, 1)
+    act.wait_ge(S.sco, NG)
+    act.wait_ge(S.nm1, 1)
+    act.activation(T.p1q[:, :], T.sco[:, 0:QP], Exp, bias=T.nm1[:, 0:1]).then_inc(S.p1q, 1)
+    if has_prev:
+        dve.tensor_reduce(T.sp[:, KP:KP + 1], T.so[:, 0:KP], X, AluOpType.max).then_inc(S.pre, 1)
+        dve.wait_ge(S.nm1, 1)
+        dve.wait_ge(S.nmask, 1)
+        dve.tensor_scalar(T.scp[:, QP:2 * QP], T.nmask[:, :], T.nm1[:, 0:1], None,
+                          AluOpType.subtract).then_inc(S.pre, 1)
+    dve.wait_ge(S.p1q, 1)
+    dve.transpose(T.p1t[:, :], T.p1q[:, :]).then_inc(S.p1t, 1)
+    pe.wait_ge(S.p1t, 1)
+    pe.wait_ge(S.ones, n_ones)
+    pe.matmul(T.o1[0:QP, 0:KP + 1], T.p1t[:, :], T.kvo[:, KP:W + 1], True, True).then_inc(S.o1, 1)
+    dve.wait_ge(S.o1, 1)
+
+    if has_prev:
+        dve.tensor_copy(T.o1b[0:QP, 0:KP + 1], T.o1[0:QP, 0:KP + 1]).then_inc(S.o1b, 1)
+        src = T.cores[rank - 1]
+        _, ne_in = _engines(topo.mask(src, core), SEND_ENGINES)
+        pe.wait_ge(S.pre, 2)
+        pe.wait_ge(S.arr, ne_in)
+        pe.matmul(T.sp[:, 0:KP], T.q4[:, :], T.kvp[:, 0:KP], True, True).then_inc(S.sp, 1)
+        for a in range(NG):
+            pe.matmul(T.scp[a * QP:(a + 1) * QP, 0:QP], T.q4[:, 0:QP], T.kvp[:, a * QP:(a + 1) * QP],
+                      True, True).then_inc(S.scp, 1)
+        dve.wait_ge(S.pre, 2)
+        dve.wait_ge(S.sp, 1)
+        dve.tensor_reduce(T.nm[:, 0:1], T.sp[:, 0:KP + 1], X, AluOpType.max, negate=True).then_inc(S.nm, 1)
+        act.wait_ge(S.pre, 2)
+        act.wait_ge(S.scp, NG)
+        act.wait_ge(S.nm, 1)
+        act.activation(T.pq[:, :], T.scp[:, 0:2 * QP], Exp, bias=T.nm[:, 0:1]).then_inc(S.pq, 1)
+        pe.wait_ge(S.o1b, 1)
+        pe.wait_ge(S.pq, 1)
+        pe.matmul(T.o[0:QP, 0:KP + 1], T.pq[0:QP, QP:2 * QP], T.o1b[0:QP, 0:KP + 1], True, False)
+        dve.wait_ge(S.pq, 1)
+        dve.transpose(T.pt[:, :], T.pq[:, 0:QP]).then_inc(S.pt, 1)
+        pe.wait_ge(S.pt, 1)
+        pe.matmul(T.o[0:QP, 0:KP + 1], T.pt[:, :], T.kvp[:, KP:W + 1], False, True).then_inc(S.o, 1)
+        dve.wait_ge(S.o, 1)
+        acc = T.o
+    else:
+        acc = T.o1
+
+    dve.reciprocal(T.rl[0:QP, 0:1], acc[0:QP, KP:KP + 1]).then_inc(S.rl, 1)
+    dve.wait_ge(S.rl, 1)
+    dve.tensor_scalar(T.ysb[0:QP, :], acc[0:QP, 0:KP], T.rl[0:QP, 0:1], None, AluOpType.mult).then_inc(S.y, 1)
+    sp.wait_ge(S.y, 1)
+    sp.dma_start(T.y[:, :], T.ysb[0:QP, :]).then_inc(S.st, 16)
+    sp.wait_ge(S.st, 16)

@@ -4,6 +4,7 @@ QP = 32
 KP = 128
 NG = KP // QP
 W = 2 * KP
+H = KP // 2
 SEND_ENGINES = 8
 FAR = -30000.0
 
@@ -27,10 +28,12 @@ SCRATCH = {
     "sp": ("psum", [128, 512], "float32"),
     "scp": ("psum", [128, 512], "float32"),
     "o1": ("psum", [128, 512], "float32"),
-    "o": ("psum", [128, 512], "float32"),
+    "oa": ("psum", [128, 512], "float32"),
+    "ob": ("psum", [128, 512], "float32"),
+    "l": ("psum", [128, 512], "float32"),
 }
-SEMAPHORES = ["kv", "q", "z", "nm0", "nmask", "ones", "q4", "so", "sco", "nm1", "pre", "p1q", "p1t", "o1", "o1b",
-              "arr", "sent", "sp", "scp", "nm", "pq", "pt", "o", "rl", "y", "st"]
+SEMAPHORES = ["k", "v", "q", "z", "nm0", "nmask", "ones", "q4", "so", "sco", "nm1", "pre", "p1q", "p1t", "o1", "o1b",
+              "arrk", "arrv", "sent", "sp", "scp", "nm", "pq", "pt", "l", "oa", "ob", "rl", "y", "st"]
 
 
 def _engines(mask, n):
@@ -54,8 +57,8 @@ def rank_program(g, core, T, topo):
     has_prev = rank > 0
     has_next = rank + 1 < n
 
-    sp.dma_start(T.kvo[:, 0:KP], T.k[:, :]).then_inc(S.kv, 16)
-    act.dma_start(T.kvo[:, KP:W], T.v[:, :]).then_inc(S.kv, 16)
+    sp.dma_start(T.kvo[:, 0:KP], T.k[:, :]).then_inc(S.k, 16)
+    act.dma_start(T.kvo[:, KP:W], T.v[:, :]).then_inc(S.v, 16)
     sp.dma_start(T.q4[:, 0:QP], T.q[:, :]).then_inc(S.q, 16)
 
     dve.memset(T.z[:, :], 0.0).then_inc(S.z, 1)
@@ -75,14 +78,16 @@ def rank_program(g, core, T, topo):
             raise ValueError("rank %d may not write to the next rank directly" % rank)
         rid, pid, _ = topo.addr(dst)
         em, ne = _engines(topo.mask(core, dst), SEND_ENGINES)
-        g.wait_ge(S.kv, 32)
-        g.remote_dma(T.kvp[:, 0:W], T.kvo[:, 0:W], S.arr, S.sent, pid, rid, em)
-        g.wait_ge(S.sent, ne)
+        g.wait_ge(S.k, 16)
+        g.remote_dma(T.kvp[:, 0:KP], T.kvo[:, 0:KP], S.arrk, S.sent, pid, rid, em)
+        g.wait_ge(S.v, 16)
+        g.remote_dma(T.kvp[:, KP:W], T.kvo[:, KP:W], S.arrv, S.sent, pid, rid, em)
+        g.wait_ge(S.sent, 2 * ne)
 
     dve.wait_ge(S.q, 16)
     for a in range(1, NG):
         dve.tensor_copy(T.q4[:, a * QP:(a + 1) * QP], T.q4[:, 0:QP]).then_inc(S.q4, 1)
-    pe.wait_ge(S.kv, 32)
+    pe.wait_ge(S.k, 16)
     pe.wait_ge(S.q, 16)
     pe.wait_ge(S.q4, NG - 1)
     pe.matmul(T.so[:, 0:KP], T.q4[:, :], T.kvo[:, 0:KP], True, True).then_inc(S.so, 1)
@@ -103,16 +108,21 @@ def rank_program(g, core, T, topo):
     dve.wait_ge(S.p1q, 1)
     dve.transpose(T.p1t[:, :], T.p1q[:, :]).then_inc(S.p1t, 1)
     pe.wait_ge(S.p1t, 1)
+    pe.wait_ge(S.v, 16)
     pe.wait_ge(S.ones, n_ones)
     pe.matmul(T.o1[0:QP, 0:KP + 1], T.p1t[:, :], T.kvo[:, KP:W + 1], True, True).then_inc(S.o1, 1)
     dve.wait_ge(S.o1, 1)
 
-    if has_prev:
+    if not has_prev:
+        dve.reciprocal(T.rl[0:QP, 0:1], T.o1[0:QP, KP:KP + 1]).then_inc(S.rl, 1)
+        dve.wait_ge(S.rl, 1)
+        dve.tensor_scalar(T.ysb[0:QP, :], T.o1[0:QP, 0:KP], T.rl[0:QP, 0:1], None, AluOpType.mult).then_inc(S.y, 2)
+    else:
         dve.tensor_copy(T.o1b[0:QP, 0:KP + 1], T.o1[0:QP, 0:KP + 1]).then_inc(S.o1b, 1)
-        src = T.cores[rank - 1]
-        _, ne_in = _engines(topo.mask(src, core), SEND_ENGINES)
+        _, ne_in = _engines(topo.mask(T.cores[rank - 1], core), SEND_ENGINES)
+        diag = T.pq[0:QP, QP:2 * QP]
         pe.wait_ge(S.pre, 2)
-        pe.wait_ge(S.arr, ne_in)
+        pe.wait_ge(S.arrk, ne_in)
         pe.matmul(T.sp[:, 0:KP], T.q4[:, :], T.kvp[:, 0:KP], True, True).then_inc(S.sp, 1)
         for a in range(NG):
             pe.matmul(T.scp[a * QP:(a + 1) * QP, 0:QP], T.q4[:, 0:QP], T.kvp[:, a * QP:(a + 1) * QP],
@@ -124,21 +134,26 @@ def rank_program(g, core, T, topo):
         act.wait_ge(S.scp, NG)
         act.wait_ge(S.nm, 1)
         act.activation(T.pq[:, :], T.scp[:, 0:2 * QP], Exp, bias=T.nm[:, 0:1]).then_inc(S.pq, 1)
-        pe.wait_ge(S.o1b, 1)
-        pe.wait_ge(S.pq, 1)
-        pe.matmul(T.o[0:QP, 0:KP + 1], T.pq[0:QP, QP:2 * QP], T.o1b[0:QP, 0:KP + 1], True, False)
         dve.wait_ge(S.pq, 1)
         dve.transpose(T.pt[:, :], T.pq[:, 0:QP]).then_inc(S.pt, 1)
+        pe.wait_ge(S.o1b, 1)
+        pe.wait_ge(S.pq, 1)
+        pe.matmul(T.l[0:QP, 0:1], diag, T.o1b[0:QP, KP:KP + 1], True, False)
         pe.wait_ge(S.pt, 1)
-        pe.matmul(T.o[0:QP, 0:KP + 1], T.pt[:, :], T.kvp[:, KP:W + 1], False, True).then_inc(S.o, 1)
-        dve.wait_ge(S.o, 1)
-        acc = T.o
-    else:
-        acc = T.o1
+        pe.matmul(T.l[0:QP, 0:1], T.pt[:, :], T.kvp[:, W:W + 1], False, True).then_inc(S.l, 1)
+        pe.matmul(T.oa[0:QP, 0:H], diag, T.o1b[0:QP, 0:H], True, False)
+        pe.matmul(T.ob[0:QP, 0:H], diag, T.o1b[0:QP, H:KP], True, False)
+        dve.wait_ge(S.l, 1)
+        dve.reciprocal(T.rl[0:QP, 0:1], T.l[0:QP, 0:1]).then_inc(S.rl, 1)
+        pe.wait_ge(S.arrv, ne_in)
+        pe.matmul(T.oa[0:QP, 0:H], T.pt[:, :], T.kvp[:, KP:KP + H], False, True).then_inc(S.oa, 1)
+        pe.matmul(T.ob[0:QP, 0:H], T.pt[:, :], T.kvp[:, KP + H:W], False, True).then_inc(S.ob, 1)
+        dve.wait_ge(S.rl, 1)
+        dve.wait_ge(S.oa, 1)
+        dve.tensor_scalar(T.ysb[0:QP, 0:H], T.oa[0:QP, 0:H], T.rl[0:QP, 0:1], None, AluOpType.mult).then_inc(S.y, 1)
+        dve.wait_ge(S.ob, 1)
+        dve.tensor_scalar(T.ysb[0:QP, H:KP], T.ob[0:QP, 0:H], T.rl[0:QP, 0:1], None, AluOpType.mult).then_inc(S.y, 1)
 
-    dve.reciprocal(T.rl[0:QP, 0:1], acc[0:QP, KP:KP + 1]).then_inc(S.rl, 1)
-    dve.wait_ge(S.rl, 1)
-    dve.tensor_scalar(T.ysb[0:QP, :], acc[0:QP, 0:KP], T.rl[0:QP, 0:1], None, AluOpType.mult).then_inc(S.y, 1)
-    sp.wait_ge(S.y, 1)
+    sp.wait_ge(S.y, 2)
     sp.dma_start(T.y[:, :], T.ysb[0:QP, :]).then_inc(S.st, 16)
     sp.wait_ge(S.st, 16)

@@ -10,9 +10,10 @@ FAR = -30000.0
 
 SCRATCH = {
     "kvo": ("sbuf", [128, W + 8], "bfloat16"),
-    "kvp": ("sbuf", [128, W + 8], "bfloat16"),
+    "kvp": ("sbuf", [128, W], "bfloat16"),
     "q4": ("sbuf", [128, NG * QP], "bfloat16"),
     "z": ("sbuf", [128, 8], "bfloat16"),
+    "fz": ("sbuf", [128, QP], "float32"),
     "nmask": ("sbuf", [128, QP], "float32"),
     "nm1": ("sbuf", [128, 4], "float32"),
     "nm": ("sbuf", [128, 4], "float32"),
@@ -20,17 +21,17 @@ SCRATCH = {
     "p1t": ("sbuf", [128, QP], "bfloat16"),
     "pq": ("sbuf", [128, 2 * QP], "bfloat16"),
     "pt": ("sbuf", [128, QP], "bfloat16"),
-    "o1b": ("sbuf", [128, KP + 8], "bfloat16"),
+    "o1b": ("sbuf", [128, KP], "bfloat16"),
+    "pf": ("sbuf", [128, W], "bfloat16"),
+    "ls": ("sbuf", [128, 4], "float32"),
     "rl": ("sbuf", [128, 4], "float32"),
     "ysb": ("sbuf", [128, KP], "bfloat16"),
-    "so": ("psum", [128, 512], "float32"),
-    "sco": ("psum", [128, 512], "float32"),
     "sp": ("psum", [128, 512], "float32"),
+    "sco": ("psum", [128, 512], "float32"),
     "scp": ("psum", [128, 512], "float32"),
     "o1": ("psum", [128, 512], "float32"),
     "oa": ("psum", [128, 512], "float32"),
     "ob": ("psum", [128, 512], "float32"),
-    "l": ("psum", [128, 512], "float32"),
 }
 SEMAPHORES = ["k", "v", "q", "z", "nm0", "nmask", "ones", "q4", "so", "sco", "nm1", "pre", "p1q", "p1t", "o1", "o1b",
               "arrk", "arrv", "sent", "sp", "scp", "nm", "pq", "pt", "l", "oa", "ob", "rl", "y", "st"]
@@ -61,16 +62,14 @@ def rank_program(g, core, T, topo):
     act.dma_start(T.kvo[:, KP:W], T.v[:, :]).then_inc(S.v, 16)
     sp.dma_start(T.q4[:, 0:QP], T.q[:, :]).then_inc(S.q, 16)
 
-    dve.memset(T.z[:, :], 0.0).then_inc(S.z, 1)
-    act.wait_ge(S.z, 1)
-    act.activation(T.kvo[:, W:W + 8], T.z[:, :], Exp).then_inc(S.ones, 1)
-    n_ones = 1
     if has_prev:
-        act.activation(T.kvp[:, W:W + 8], T.z[:, :], Exp).then_inc(S.ones, 1)
-        n_ones = 2
-        dve.memset(T.nmask[:, :], 0.0).then_inc(S.nm0, 1)
-        g.wait_ge(S.nm0, 1)
-        g.affine_select(T.nmask[:, :], T.nmask[:, :], [[-1, QP]], AluOpType.is_equal, FAR, 0, 1).then_inc(S.nmask, 1)
+        dve.memset(T.fz[:, :], FAR).then_inc(S.z, 1)
+        act.wait_ge(S.z, 1)
+        act.activation(T.nmask[:, :], T.fz[:, :], Exp).then_inc(S.nm0, 1)
+    else:
+        dve.memset(T.z[:, :], 0.0).then_inc(S.z, 1)
+        act.wait_ge(S.z, 1)
+        act.activation(T.kvo[:, W:W + 8], T.z[:, :], Exp).then_inc(S.ones, 1)
 
     if has_next:
         dst = T.cores[rank + 1]
@@ -80,6 +79,10 @@ def rank_program(g, core, T, topo):
         em, ne = _engines(topo.mask(core, dst), SEND_ENGINES)
         g.wait_ge(S.k, 16)
         g.remote_dma(T.kvp[:, 0:KP], T.kvo[:, 0:KP], S.arrk, S.sent, pid, rid, em)
+    if has_prev:
+        g.wait_ge(S.nm0, 1)
+        g.affine_select(T.nmask[:, :], T.nmask[:, :], [[-1, QP]], AluOpType.is_equal, FAR, 0, 1).then_inc(S.nmask, 1)
+    if has_next:
         g.wait_ge(S.v, 16)
         g.remote_dma(T.kvp[:, KP:W], T.kvo[:, KP:W], S.arrv, S.sent, pid, rid, em)
         g.wait_ge(S.sent, 2 * ne)
@@ -90,69 +93,75 @@ def rank_program(g, core, T, topo):
     pe.wait_ge(S.k, 16)
     pe.wait_ge(S.q, 16)
     pe.wait_ge(S.q4, NG - 1)
-    pe.matmul(T.so[:, 0:KP], T.q4[:, :], T.kvo[:, 0:KP], True, True).then_inc(S.so, 1)
+    pe.matmul(T.sp[:, 0:KP], T.q4[:, :], T.kvo[:, 0:KP], True, True).then_inc(S.so, 1)
     for a in range(NG):
         pe.matmul(T.sco[a * QP:(a + 1) * QP, 0:QP], T.q4[:, 0:QP], T.kvo[:, a * QP:(a + 1) * QP],
                   True, True).then_inc(S.sco, 1)
     dve.wait_ge(S.so, 1)
-    dve.tensor_reduce(T.nm1[:, 0:1], T.so[:, 0:KP], X, AluOpType.max, negate=True).then_inc(S.nm1, 1)
+    dve.tensor_reduce(T.nm1[:, 0:1], T.sp[:, 0:KP], X, AluOpType.max, negate=True).then_inc(S.nm1, 1)
     act.wait_ge(S.sco, NG)
     act.wait_ge(S.nm1, 1)
     act.activation(T.p1q[:, :], T.sco[:, 0:QP], Exp, bias=T.nm1[:, 0:1]).then_inc(S.p1q, 1)
     if has_prev:
-        dve.tensor_reduce(T.sp[:, KP:KP + 1], T.so[:, 0:KP], X, AluOpType.max).then_inc(S.pre, 1)
-        dve.wait_ge(S.nm1, 1)
-        dve.wait_ge(S.nmask, 1)
-        dve.tensor_scalar(T.scp[:, QP:2 * QP], T.nmask[:, :], T.nm1[:, 0:1], None,
-                          AluOpType.subtract).then_inc(S.pre, 1)
+        dve.tensor_reduce(T.sp[:, W:W + 1], T.sp[:, 0:KP], X, AluOpType.max).then_inc(S.pre, 1)
     dve.wait_ge(S.p1q, 1)
     dve.transpose(T.p1t[:, :], T.p1q[:, :]).then_inc(S.p1t, 1)
     pe.wait_ge(S.p1t, 1)
     pe.wait_ge(S.v, 16)
-    pe.wait_ge(S.ones, n_ones)
-    pe.matmul(T.o1[0:QP, 0:KP + 1], T.p1t[:, :], T.kvo[:, KP:W + 1], True, True).then_inc(S.o1, 1)
-    dve.wait_ge(S.o1, 1)
 
     if not has_prev:
+        pe.wait_ge(S.ones, 1)
+        pe.matmul(T.o1[0:QP, 0:KP + 1], T.p1t[:, :], T.kvo[:, KP:W + 1], True, True).then_inc(S.o1, 1)
+        dve.wait_ge(S.o1, 1)
         dve.reciprocal(T.rl[0:QP, 0:1], T.o1[0:QP, KP:KP + 1]).then_inc(S.rl, 1)
         dve.wait_ge(S.rl, 1)
         dve.tensor_scalar(T.ysb[0:QP, :], T.o1[0:QP, 0:KP], T.rl[0:QP, 0:1], None, AluOpType.mult).then_inc(S.y, 2)
     else:
-        dve.tensor_copy(T.o1b[0:QP, 0:KP + 1], T.o1[0:QP, 0:KP + 1]).then_inc(S.o1b, 1)
+        pe.matmul(T.o1[0:QP, 0:KP], T.p1t[:, :], T.kvo[:, KP:W], True, True).then_inc(S.o1, 1)
+        dve.wait_ge(S.o1, 1)
+        dve.tensor_copy(T.o1b[0:QP, :], T.o1[0:QP, 0:KP]).then_inc(S.o1b, 1)
+        dve.wait_ge(S.nm1, 1)
+        dve.wait_ge(S.nmask, 1)
+        dve.tensor_scalar(T.scp[:, QP:2 * QP], T.nmask[:, :], T.nm1[:, 0:1], None,
+                          AluOpType.subtract).then_inc(S.pre, 1)
         _, ne_in = _engines(topo.mask(T.cores[rank - 1], core), SEND_ENGINES)
         diag = T.pq[0:QP, QP:2 * QP]
         pe.wait_ge(S.pre, 2)
         pe.wait_ge(S.arrk, ne_in)
-        pe.matmul(T.sp[:, 0:KP], T.q4[:, :], T.kvp[:, 0:KP], True, True).then_inc(S.sp, 1)
+        pe.matmul(T.sp[:, KP:W], T.q4[:, :], T.kvp[:, 0:KP], True, True).then_inc(S.sp, 1)
         for a in range(NG):
             pe.matmul(T.scp[a * QP:(a + 1) * QP, 0:QP], T.q4[:, 0:QP], T.kvp[:, a * QP:(a + 1) * QP],
                       True, True).then_inc(S.scp, 1)
         dve.wait_ge(S.pre, 2)
         dve.wait_ge(S.sp, 1)
-        dve.tensor_reduce(T.nm[:, 0:1], T.sp[:, 0:KP + 1], X, AluOpType.max, negate=True).then_inc(S.nm, 1)
+        dve.tensor_reduce(T.nm[:, 0:1], T.sp[:, KP:W + 1], X, AluOpType.max, negate=True).then_inc(S.nm, 1)
         act.wait_ge(S.pre, 2)
         act.wait_ge(S.scp, NG)
         act.wait_ge(S.nm, 1)
         act.activation(T.pq[:, :], T.scp[:, 0:2 * QP], Exp, bias=T.nm[:, 0:1]).then_inc(S.pq, 1)
+        act.wait_ge(S.so, 1)
+        act.wait_ge(S.sp, 1)
+        act.activation(T.pf[0:QP, :], T.sp[0:QP, 0:W], Exp, bias=T.nm[0:QP, 0:1],
+                       accum_out=T.ls[0:QP, 0:1]).then_inc(S.l, 1)
         dve.wait_ge(S.pq, 1)
         dve.transpose(T.pt[:, :], T.pq[:, 0:QP]).then_inc(S.pt, 1)
+        dve.wait_ge(S.l, 1)
+        dve.reciprocal(T.rl[0:QP, 0:1], T.ls[0:QP, 0:1]).then_inc(S.rl, 1)
         pe.wait_ge(S.o1b, 1)
         pe.wait_ge(S.pq, 1)
-        pe.matmul(T.l[0:QP, 0:1], diag, T.o1b[0:QP, KP:KP + 1], True, False)
-        pe.wait_ge(S.pt, 1)
-        pe.matmul(T.l[0:QP, 0:1], T.pt[:, :], T.kvp[:, W:W + 1], False, True).then_inc(S.l, 1)
         pe.matmul(T.oa[0:QP, 0:H], diag, T.o1b[0:QP, 0:H], True, False)
         pe.matmul(T.ob[0:QP, 0:H], diag, T.o1b[0:QP, H:KP], True, False)
-        dve.wait_ge(S.l, 1)
-        dve.reciprocal(T.rl[0:QP, 0:1], T.l[0:QP, 0:1]).then_inc(S.rl, 1)
+        pe.wait_ge(S.pt, 1)
         pe.wait_ge(S.arrv, ne_in)
         pe.matmul(T.oa[0:QP, 0:H], T.pt[:, :], T.kvp[:, KP:KP + H], False, True).then_inc(S.oa, 1)
         pe.matmul(T.ob[0:QP, 0:H], T.pt[:, :], T.kvp[:, KP + H:W], False, True).then_inc(S.ob, 1)
         dve.wait_ge(S.rl, 1)
         dve.wait_ge(S.oa, 1)
         dve.tensor_scalar(T.ysb[0:QP, 0:H], T.oa[0:QP, 0:H], T.rl[0:QP, 0:1], None, AluOpType.mult).then_inc(S.y, 1)
-        dve.wait_ge(S.ob, 1)
-        dve.tensor_scalar(T.ysb[0:QP, H:KP], T.ob[0:QP, 0:H], T.rl[0:QP, 0:1], None, AluOpType.mult).then_inc(S.y, 1)
+        act.wait_ge(S.rl, 1)
+        act.wait_ge(S.ob, 1)
+        act.activation(T.ysb[0:QP, H:KP], T.ob[0:QP, 0:H], ActivationFunctionType.Copy,
+                       scale=T.rl[0:QP, 0:1]).then_inc(S.y, 1)
 
     sp.wait_ge(S.y, 2)
     sp.dma_start(T.y[:, :], T.ysb[0:QP, :]).then_inc(S.st, 16)

from concourse.mybir import AluOpType, AxisListType, ActivationFunctionType

QP = 32
KP = 128
NG = KP // QP
W = 2 * KP
H = KP // 2
SEND_ENGINES = 8
FAR = -30000.0

SCRATCH = {
    "kvo": ("sbuf", [128, W + 8], "bfloat16"),
    "kvp": ("sbuf", [128, W], "bfloat16"),
    "q4": ("sbuf", [128, NG * QP], "bfloat16"),
    "z": ("sbuf", [128, 8], "bfloat16"),
    "fz": ("sbuf", [128, QP], "float32"),
    "nmask": ("sbuf", [128, QP], "float32"),
    "nm1": ("sbuf", [128, 4], "float32"),
    "nm": ("sbuf", [128, 4], "float32"),
    "p1q": ("sbuf", [128, QP], "bfloat16"),
    "p1t": ("sbuf", [128, QP], "bfloat16"),
    "pq": ("sbuf", [128, 2 * QP], "bfloat16"),
    "pt": ("sbuf", [128, QP], "bfloat16"),
    "o1b": ("sbuf", [128, KP], "bfloat16"),
    "pf": ("sbuf", [128, W], "bfloat16"),
    "ls": ("sbuf", [128, 4], "float32"),
    "rl": ("sbuf", [128, 4], "float32"),
    "ysb": ("sbuf", [128, KP], "bfloat16"),
    "sp": ("psum", [128, 512], "float32"),
    "sco": ("psum", [128, 512], "float32"),
    "scp": ("psum", [128, 512], "float32"),
    "o1": ("psum", [128, 512], "float32"),
    "oa": ("psum", [128, 512], "float32"),
    "ob": ("psum", [128, 512], "float32"),
}
SEMAPHORES = ["k", "v", "q", "z", "nm0", "nmask", "ones", "q4", "so", "sco", "nm1", "pre", "p1q", "p1t", "o1", "o1b",
              "arrk", "arrv", "sent", "sp", "scp", "nm", "pq", "pt", "l", "oa", "ob", "rl", "y", "st"]


def _engines(mask, n):
    out, cnt = 0, 0
    for b in range(mask.bit_length()):
        if (mask >> b) & 1 and cnt < n:
            out |= 1 << b
            cnt += 1
    return out, cnt


def rank_program(g, core, T, topo):
    rank = T.rank_of(core)
    if rank is None:
        return
    S = T.sem
    pe, dve, act, sp = g.tensor, g.vector, g.scalar, g.sync
    Exp = ActivationFunctionType.Exp
    X = AxisListType.X
    n = len(T.cores)
    has_prev = rank > 0
    has_next = rank + 1 < n

    sp.dma_start(T.kvo[:, 0:KP], T.k[:, :]).then_inc(S.k, 16)
    act.dma_start(T.kvo[:, KP:W], T.v[:, :]).then_inc(S.v, 16)
    sp.dma_start(T.q4[:, 0:QP], T.q[:, :]).then_inc(S.q, 16)

    if has_prev:
        dve.memset(T.fz[:, :], FAR).then_inc(S.z, 1)
        act.wait_ge(S.z, 1)
        act.activation(T.nmask[:, :], T.fz[:, :], Exp).then_inc(S.nm0, 1)
    else:
        dve.memset(T.z[:, :], 0.0).then_inc(S.z, 1)
        act.wait_ge(S.z, 1)
        act.activation(T.kvo[:, W:W + 8], T.z[:, :], Exp).then_inc(S.ones, 1)

    if has_next:
        dst = T.cores[rank + 1]
        if not topo.may_write(core, dst):
            raise ValueError("rank %d may not write to the next rank directly" % rank)
        rid, pid, _ = topo.addr(dst)
        em, ne = _engines(topo.mask(core, dst), SEND_ENGINES)
        g.wait_ge(S.k, 16)
        g.remote_dma(T.kvp[:, 0:KP], T.kvo[:, 0:KP], S.arrk, S.sent, pid, rid, em)
    if has_prev:
        g.wait_ge(S.nm0, 1)
        g.affine_select(T.nmask[:, :], T.nmask[:, :], [[-1, QP]], AluOpType.is_equal, FAR, 0, 1).then_inc(S.nmask, 1)
    if has_next:
        g.wait_ge(S.v, 16)
        g.remote_dma(T.kvp[:, KP:W], T.kvo[:, KP:W], S.arrv, S.sent, pid, rid, em)
        g.wait_ge(S.sent, 2 * ne)

    dve.wait_ge(S.q, 16)
    for a in range(1, NG):
        dve.tensor_copy(T.q4[:, a * QP:(a + 1) * QP], T.q4[:, 0:QP]).then_inc(S.q4, 1)
    pe.wait_ge(S.k, 16)
    pe.wait_ge(S.q, 16)
    pe.wait_ge(S.q4, NG - 1)
    pe.matmul(T.sp[:, 0:KP], T.q4[:, :], T.kvo[:, 0:KP], True, True).then_inc(S.so, 1)
    for a in range(NG):
        pe.matmul(T.sco[a * QP:(a + 1) * QP, 0:QP], T.q4[:, 0:QP], T.kvo[:, a * QP:(a + 1) * QP],
                  True, True).then_inc(S.sco, 1)
    dve.wait_ge(S.so, 1)
    dve.tensor_reduce(T.nm1[:, 0:1], T.sp[:, 0:KP], X, AluOpType.max, negate=True).then_inc(S.nm1, 1)
    act.wait_ge(S.sco, NG)
    act.wait_ge(S.nm1, 1)
    act.activation(T.p1q[:, :], T.sco[:, 0:QP], Exp, bias=T.nm1[:, 0:1]).then_inc(S.p1q, 1)
    if has_prev:
        dve.tensor_reduce(T.sp[:, W:W + 1], T.sp[:, 0:KP], X, AluOpType.max).then_inc(S.pre, 1)
    dve.wait_ge(S.p1q, 1)
    dve.transpose(T.p1t[:, :], T.p1q[:, :]).then_inc(S.p1t, 1)
    pe.wait_ge(S.p1t, 1)
    pe.wait_ge(S.v, 16)

    if not has_prev:
        pe.wait_ge(S.ones, 1)
        pe.matmul(T.o1[0:QP, 0:KP + 1], T.p1t[:, :], T.kvo[:, KP:W + 1], True, True).then_inc(S.o1, 1)
        dve.wait_ge(S.o1, 1)
        dve.reciprocal(T.rl[0:QP, 0:1], T.o1[0:QP, KP:KP + 1]).then_inc(S.rl, 1)
        dve.wait_ge(S.rl, 1)
        dve.tensor_scalar(T.ysb[0:QP, :], T.o1[0:QP, 0:KP], T.rl[0:QP, 0:1], None, AluOpType.mult).then_inc(S.y, 2)
    else:
        pe.matmul(T.o1[0:QP, 0:KP], T.p1t[:, :], T.kvo[:, KP:W], True, True).then_inc(S.o1, 1)
        dve.wait_ge(S.o1, 1)
        dve.tensor_copy(T.o1b[0:QP, :], T.o1[0:QP, 0:KP]).then_inc(S.o1b, 1)
        dve.wait_ge(S.nm1, 1)
        dve.wait_ge(S.nmask, 1)
        dve.tensor_scalar(T.scp[:, QP:2 * QP], T.nmask[:, :], T.nm1[:, 0:1], None,
                          AluOpType.subtract).then_inc(S.pre, 1)
        _, ne_in = _engines(topo.mask(T.cores[rank - 1], core), SEND_ENGINES)
        diag = T.pq[0:QP, QP:2 * QP]
        pe.wait_ge(S.pre, 2)
        pe.wait_ge(S.arrk, ne_in)
        pe.matmul(T.sp[:, KP:W], T.q4[:, :], T.kvp[:, 0:KP], True, True).then_inc(S.sp, 1)
        for a in range(NG):
            pe.matmul(T.scp[a * QP:(a + 1) * QP, 0:QP], T.q4[:, 0:QP], T.kvp[:, a * QP:(a + 1) * QP],
                      True, True).then_inc(S.scp, 1)
        dve.wait_ge(S.pre, 2)
        dve.wait_ge(S.sp, 1)
        dve.tensor_reduce(T.nm[:, 0:1], T.sp[:, KP:W + 1], X, AluOpType.max, negate=True).then_inc(S.nm, 1)
        act.wait_ge(S.pre, 2)
        act.wait_ge(S.scp, NG)
        act.wait_ge(S.nm, 1)
        act.activation(T.pq[:, :], T.scp[:, 0:2 * QP], Exp, bias=T.nm[:, 0:1]).then_inc(S.pq, 1)
        act.wait_ge(S.so, 1)
        act.wait_ge(S.sp, 1)
        act.activation(T.pf[0:QP, :], T.sp[0:QP, 0:W], Exp, bias=T.nm[0:QP, 0:1],
                       accum_out=T.ls[0:QP, 0:1]).then_inc(S.l, 1)
        dve.wait_ge(S.pq, 1)
        dve.transpose(T.pt[:, :], T.pq[:, 0:QP]).then_inc(S.pt, 1)
        dve.wait_ge(S.l, 1)
        dve.reciprocal(T.rl[0:QP, 0:1], T.ls[0:QP, 0:1]).then_inc(S.rl, 1)
        pe.wait_ge(S.o1b, 1)
        pe.wait_ge(S.pq, 1)
        pe.matmul(T.oa[0:QP, 0:H], diag, T.o1b[0:QP, 0:H], True, False)
        pe.matmul(T.ob[0:QP, 0:H], diag, T.o1b[0:QP, H:KP], True, False)
        pe.wait_ge(S.pt, 1)
        pe.wait_ge(S.arrv, ne_in)
        pe.matmul(T.oa[0:QP, 0:H], T.pt[:, :], T.kvp[:, KP:KP + H], False, True).then_inc(S.oa, 1)
        pe.matmul(T.ob[0:QP, 0:H], T.pt[:, :], T.kvp[:, KP + H:W], False, True).then_inc(S.ob, 1)
        dve.wait_ge(S.rl, 1)
        dve.wait_ge(S.oa, 1)
        dve.tensor_scalar(T.ysb[0:QP, 0:H], T.oa[0:QP, 0:H], T.rl[0:QP, 0:1], None, AluOpType.mult).then_inc(S.y, 1)
        act.wait_ge(S.rl, 1)
        act.wait_ge(S.ob, 1)
        act.activation(T.ysb[0:QP, H:KP], T.ob[0:QP, 0:H], ActivationFunctionType.Copy,
                       scale=T.rl[0:QP, 0:1]).then_inc(S.y, 1)

    sp.wait_ge(S.y, 2)
    sp.dma_start(T.y[:, :], T.ysb[0:QP, :]).then_inc(S.st, 16)
    sp.wait_ge(S.st, 16)
